import numpy as np
import ml_dtypes


def mxq(x, axis, fmt="e4m3"):
    dtype, down = {"e4m3": (ml_dtypes.float8_e4m3fn, 7), "e5m2": (ml_dtypes.float8_e5m2, 14)}[fmt]
    v = np.moveaxis(np.asarray(x, np.float32).astype(ml_dtypes.bfloat16).astype(np.float64), axis, -1)
    blocks = v.reshape(v.shape[:-1] + (-1, 32))
    amax = np.abs(blocks).max(-1, keepdims=True)
    byte = np.maximum(np.where(amax > 0, np.frexp(amax)[1] - 1 + 127, 0) - down, 1)
    scale = np.exp2(byte - 127.0)
    codes = (blocks / scale).astype(np.float32).astype(dtype).astype(np.float64)
    return np.moveaxis((codes * scale).reshape(v.shape), -1, axis)


WIDE = False


def mx_kscale(k):
    if not WIDE:
        return np.ones(k)
    levels = np.array([10, -10, 5, -5, 0])
    if k % 512:
        return np.exp2(np.random.permutation(np.resize(levels, k // 32))).repeat(32)
    a = np.empty((k // 512, 16))
    for p in range(k // 512):
        a[p, :8] = np.random.permutation(np.resize(levels, 8))
        for g in range(8):
            far = levels[np.abs(levels - a[p, g]) >= 10]
            a[p, g + 8] = far[np.random.randint(len(far))]
    return np.exp2(a.ravel()).repeat(32)


def f64(x):
    return np.asarray(x).astype(np.float64)


def striped(idx):
    return np.tile(idx.reshape(-1, 16).T, (8, 1)).astype(np.uint16)


def unstriped(offs):
    return offs[:16].T.reshape(-1).astype(np.int64)


def striped8(idx):
    return np.concatenate([x.reshape(-1, 16).T for x in idx]).astype(np.uint16)


def runs(offs, k):
    lists = np.stack([offs[16 * r : 16 * r + 16].T.reshape(-1) for r in range(8)]).astype(np.int64)
    return lists[np.arange(k) % 512 // 64]


def pack_weight(w):
    k, n = w.shape
    w = f64(np.asarray(w, np.float32).astype(ml_dtypes.bfloat16)).reshape(k // 32, 32, n)
    amax = np.abs(w).max(1)
    byte = np.clip(np.where(amax > 0, np.frexp(amax)[1] - 1 + 127 - 7, 1), 1, 254)
    scaled = (w * np.exp2(127.0 - byte)[:, None, :]).reshape(k, n).astype(np.float32)
    words = np.ascontiguousarray(scaled.reshape(k // 512, 128, 4, n).transpose(0, 1, 3, 2)).astype(ml_dtypes.float8_e4m3fn).view(np.uint8)
    return words, np.ascontiguousarray(byte.astype(np.uint8).reshape(k // 512, 16, n))


def unpack_weight(words, scales):
    g, p, n, _ = words.shape
    vals = np.ascontiguousarray(words).view(ml_dtypes.float8_e4m3fn).astype(np.float64) * np.repeat(np.exp2(scales.astype(np.float64) - 127.0), 8, axis=1)[..., None]
    return vals.transpose(0, 1, 3, 2).reshape(g * 512, n)


def sigmoid(v):
    return 1.0 / (1.0 + np.exp(-np.maximum(v, -700.0)))


K, T, S, N, H, U = 512, 2048, 512, 512, 512, 1024


def setup_inputs():
    n = np.random.standard_normal
    s = mx_kscale(K)[:, None]
    u = mx_kscale(H)
    packed_xT = pack_weight(n((K, T)) * s)
    return {
        "x_words": packed_xT[0],
        "x_scales": packed_xT[1],
        "w1": (n((K, H)) / np.sqrt(K) / s).astype(np.float32),
        "w2": (n((K, H)) / np.sqrt(K) / s).astype(np.float32),
        "gn": (np.random.uniform(0.5, 1.5, (H, 1)) * u[:, None]).astype(np.float32),
        "w3": (n((H, N)) / np.sqrt(H) / u[:, None]).astype(np.float32),
        "mem": n((N, U)).astype(np.float32),
        "offs": striped(np.random.permutation(T)[:S]),
        "hz": striped8(np.random.randint(0, T, (8, S))),
        "n1": striped(np.random.permutation(S)),
        "n2": striped(np.random.permutation(S)),
        "n3": striped8(np.stack([np.random.permutation(U)[:S] for _ in range(8)])),
        "n4": striped8(np.stack([np.random.permutation(U) for _ in range(8)])),
    }


def reference(x_words, x_scales, w1, w2, gn, w3, mem, offs, hz, n1, n2, n3, n4):
    xq = unpack_weight(x_words, x_scales)[:, unstriped(offs)]
    y = mxq(f64(w1), 0, "e4m3").T @ xq
    x_hz = unpack_weight(x_words, x_scales)[np.arange(K)[:, None], runs(hz, K)]
    d = mxq(f64(w2), 0, "e4m3").T @ x_hz
    z = f64(gn) * (y + (sigmoid(d[:, unstriped(n2)] - d)) * (y[:, unstriped(n1)] - y))
    h = mxq(f64(w3), 0, "e4m3").T @ mxq(z, 0, "e4m3")
    pg = f64(mem).copy()
    pg[np.arange(N)[:, None], runs(n3, N)] = h
    return pg - (0.5 * (pg[np.arange(N)[:, None], runs(n4, N)]))

@@ -1,0 +1,264 @@
+from contextlib import ExitStack
+
+import concourse.mybir as mybir
+
+K, T, S, N, H, U = 512, 2048, 512, 512, 512, 1024
+FLOPS = 3 * 2 * 512 * 512 * 512
+
+F32 = mybir.dt.float32
+BF16 = mybir.dt.bfloat16
+I32 = mybir.dt.int32
+U32 = mybir.dt.uint32
+U16 = mybir.dt.uint16
+U8 = mybir.dt.uint8
+FP8X4 = mybir.dt.float8_e4m3fn_x4
+ACT = mybir.ActivationFunctionType
+ALU = mybir.AluOpType
+
+P = 128
+PACK = 4
+WIDE = 256
+SCALE_ROW0 = 14
+SHIFT_ROWS = 112
+HALF_U = U // 2
+
+
+def tile_picked_twhpullbpagem_none_p_kernel(tc, x_words, x_scales, w1, w2, gn, w3, mem, offs, hz, n1, n2, n3, n4, out):
+    nc = tc.nc
+    with ExitStack() as ctx:
+        keep = ctx.enter_context(tc.tile_pool(name="keep", bufs=1))
+        psum = ctx.enter_context(tc.psum_pool(name="psum", bufs=8))
+
+        def sb(name, shape, dtype):
+            return keep.tile(shape, dtype, name=name, align_bytes=64)
+
+        def load_list(name, src):
+            tile = keep.tile(list(src.shape), U16, name=name)
+            nc.sync.dma_start(tile[:], src)
+            return tile
+
+        def load_weight_half(name, w, half):
+            raw = sb(name, [P, PACK, H // 2], F32)
+            cols = slice(half * (H // 2), (half + 1) * (H // 2))
+            nc.sync.dma_start(out=raw[:], in_=w.rearrange("(p j) c -> p j c", j=PACK)[:, :, cols])
+            return raw
+
+        def deal_half(copy, dealt, raw, half):
+            dst = dealt[:].rearrange("p (a e m j) -> p a m j e", a=2, e=2, j=PACK)[:, :, half * 64:(half + 1) * 64]
+            copy(out=dst, in_=raw[:].rearrange("p j (m a e) -> p a m j e", a=2, e=2))
+
+        def quantise(name, src, width):
+            codes = sb(name + "_codes", [P, width], U32)
+            scales = sb(name + "_scales", [P, width], U8)
+            nc.vector.quantize_mx(out=codes[:].bitcast(FP8X4), scales=scales[:], in_=src)
+            return codes, scales
+
+        def product(acc, weight, t, codes, scales):
+            cols = slice(t * P, (t + 1) * P)
+            nc.tensor.matmul_mx(out=acc, lhsT=weight[0][:, cols].bitcast(FP8X4), lhsT_scale=weight[1][:, cols],
+                                rhs=codes.bitcast(FP8X4), rhs_scale=scales, start=True, stop=True)
+
+        def piece(lst, start, count):
+            return lst[:, start // 16:(start + count) // 16]
+
+        x_bytes = sb("x_bytes", [P, T], U8)
+        d_plane = sb("d_plane", [P, S], U8)
+        y_plane = sb("y_plane", [P, S], U8)
+        nc.vector.memset(x_bytes[:].bitcast(I32), 0)
+        nc.gpsimd.memset(d_plane[:].bitcast(I32), 0)
+        nc.gpsimd.memset(y_plane[:].bitcast(I32), 0)
+
+        w2_raw = [load_weight_half("w2_raw0", w2, 0)]
+        for q in range(4):
+            row = 32 * q + SCALE_ROW0
+            nc.sync.dma_start(out=x_bytes[row:row + 4, :].bitcast(I32), in_=x_scales[0][4 * q:4 * q + 4, :].bitcast(I32))
+        hz_list = load_list("hz_list", hz)
+        offs_list = load_list("offs_list", offs)
+        x_codes = sb("x_codes", [P, T], U32)
+        nc.sync.dma_start(out=x_codes[:].bitcast(I32), in_=x_words[0].rearrange("p n t -> p (n t)").bitcast(I32))
+        w2_raw.append(load_weight_half("w2_raw1", w2, 1))
+        w1_raw = [load_weight_half("w1_raw%d" % half, w1, half) for half in range(2)]
+        n2_list = load_list("n2_list", n2)
+        gain = sb("gain", [P, PACK], F32)
+        nc.sync.dma_start(out=gain[:], in_=gn.rearrange("(p t) o -> p (t o)", t=PACK))
+        n1_list = load_list("n1_list", n1)
+        w3_raw = [load_weight_half("w3_raw%d" % half, w3, half) for half in range(2)]
+        n3_list = load_list("n3_list", n3)
+        page = []
+        for t in range(PACK):
+            tile = sb("page%d" % t, [P, U], F32)
+            nc.sync.dma_start(out=tile[:], in_=mem.rearrange("(p t) w -> t p w", t=PACK)[t])
+            page.append(tile)
+        n4_list = load_list("n4_list", n4)
+
+        def gather_bytes(name, lst, plane):
+            picked = sb(name, [P, S], U8)
+            nc.vector.tensor_copy(picked[:], x_bytes[:].indirect(lst[:]))
+            nc.scalar.dma_start(out=plane[0:SHIFT_ROWS, :].bitcast(I32),
+                                in_=picked[SCALE_ROW0:SCALE_ROW0 + SHIFT_ROWS, :].bitcast(I32))
+
+        def gather_words(name, lst):
+            picked = sb(name, [P, S], U32)
+            nc.vector.tensor_copy(picked[:], x_codes[:].indirect(lst[:]))
+            return picked
+
+        def first_product(weight, words, plane):
+            banks = []
+            for t in range(PACK):
+                bank = psum.tile([P, S], F32, name="bank")
+                product(bank[:], weight, t, words[:], plane[:])
+                banks.append(bank)
+            return banks
+
+        gather_bytes("hz_bytes", hz_list, d_plane)
+        gather_bytes("offs_bytes", offs_list, y_plane)
+        hz_words = gather_words("hz_words", hz_list)
+        w2_dealt = sb("w2_dealt", [P, PACK * H], BF16)
+        deal_half(nc.scalar.copy, w2_dealt, w2_raw[0], 0)
+        deal_half(nc.scalar.copy, w2_dealt, w2_raw[1], 1)
+        d_banks = first_product(quantise("w2", w2_dealt[:], H), hz_words, d_plane)
+        offs_words = gather_words("offs_words", offs_list)
+        w1_dealt = sb("w1_dealt", [P, PACK * H], BF16)
+        deal_half(nc.scalar.copy, w1_dealt, w1_raw[0], 0)
+        deal_half(nc.vector.tensor_copy, w1_dealt, w1_raw[1], 1)
+        y_banks = first_product(quantise("w1", w1_dealt[:], H), offs_words, y_plane)
+        half_gain = sb("half_gain", [P, PACK], F32)
+        nc.scalar.activation(half_gain[:], gain[:], ACT.Copy, scale=0.5)
+
+        d_rows = [sb("d%d" % t, [P, S], F32) for t in range(PACK)]
+        y_rows = [sb("y%d" % t, [P, S], F32) for t in range(PACK)]
+        gate = [sb("gate%d" % t, [P, S], F32) for t in range(PACK)]
+        far = sb("far", [P, PACK, S], F32)
+        near = sb("near", [P, PACK, S], F32)
+
+        def fetch(dst, rows, lst, on_vector=False):
+            for c in range(2):
+                looked_up = rows[:].indirect(piece(lst, c * WIDE, WIDE))
+                if on_vector:
+                    nc.vector.tensor_copy(dst[:, c * WIDE:(c + 1) * WIDE], looked_up)
+                else:
+                    nc.scalar.activation(dst[:, c * WIDE:(c + 1) * WIDE], looked_up, ACT.Copy)
+
+        def gate_tile(t):
+            nc.scalar.copy(out=d_rows[t][:], in_=d_banks[t][:])
+            fetch(gate[t][:], d_rows[t], n2_list)
+            nc.vector.tensor_tensor(gate[t][:], gate[t][:], d_rows[t][:], ALU.subtract)
+            nc.scalar.activation(gate[t][:], gate[t][:], ACT.Tanh, scale=0.5)
+
+        def mix_tile(t):
+            if t in (3,):
+                nc.scalar.activation(y_rows[t][:], y_banks[t][:], ACT.Copy, scale=half_gain[:, t:t + 1])
+            else:
+                nc.vector.tensor_scalar(y_rows[t][:], y_banks[t][:], half_gain[:, t:t + 1], None, ALU.mult)
+            fetch(far[:, t, :], y_rows[t], n1_list, t in ())
+            nc.vector.scalar_tensor_tensor(near[:, t, :], gate[t][:], 1.0, y_rows[t][:], ALU.subtract, ALU.mult)
+            nc.vector.scalar_tensor_tensor(far[:, t, :], gate[t][:], 1.0, far[:, t, :], ALU.add, ALU.mult)
+
+        def quantise_z(c):
+            cols = slice(c * WIDE, (c + 1) * WIDE)
+            z = sb("z%d" % c, [P, PACK * WIDE], BF16)
+            nc.vector.tensor_tensor(z[:].rearrange("p (c e t) -> p c t e", e=2, t=PACK),
+                                    far[:, :, cols].rearrange("p t (c e) -> p c t e", e=2),
+                                    near[:, :, cols].rearrange("p t (c e) -> p c t e", e=2), ALU.subtract)
+            return quantise("z%d" % c, z[:], WIDE)
+
+        def project(t, z_q, c, h):
+            bank = psum.tile([P, S], F32, name="bank")
+            product(bank[:, 0:WIDE], w3_q, t, z_q[0][:], z_q[1][:])
+            nc.scalar.copy(out=h, in_=bank[:, 0:WIDE])
+
+        def write_page(t, c, h):
+            nc.vector.tensor_copy(page[t][:].indirect(piece(n3_list, c * WIDE, WIDE)), h)
+
+        def read_page(t, w0, n, fetch_on_vector, add_on_gpsimd):
+            res = sb("res%d_%d" % (t, w0), [P, n], F32)
+            looked_up = page[t][:].indirect(piece(n4_list, w0, n))
+            own = page[t][:, w0:w0 + n]
+            if fetch_on_vector:
+                nc.vector.tensor_copy(res[:], looked_up)
+                nc.vector.scalar_tensor_tensor(res[:], res[:], -0.5, own, ALU.mult, ALU.add)
+            else:
+                nc.scalar.activation(res[:], looked_up, ACT.Copy, scale=-0.5)
+                (nc.gpsimd if add_on_gpsimd else nc.vector).tensor_tensor(res[:], res[:], own, ALU.add)
+            (nc.scalar if fetch_on_vector else nc.sync).dma_start(out=out.rearrange("(p t) w -> t p w", t=PACK)[t][:, w0:w0 + n], in_=res[:])
+
+        def leave_y(t):
+            if t in (3,):
+                nc.scalar.activation(y_rows[t][:], y_banks[t][:], ACT.Copy, scale=half_gain[:, t:t + 1])
+            else:
+                nc.vector.tensor_scalar(y_rows[t][:], y_banks[t][:], half_gain[:, t:t + 1], None, ALU.mult)
+
+        def fetch_half(dst, rows, lst, c, on_vector):
+            looked_up = rows[:].indirect(piece(lst, c * WIDE, WIDE))
+            if on_vector:
+                nc.vector.tensor_copy(dst[:, c * WIDE:(c + 1) * WIDE], looked_up)
+            else:
+                nc.scalar.activation(dst[:, c * WIDE:(c + 1) * WIDE], looked_up, ACT.Copy)
+
+        def weigh_far(t, c):
+            cols = slice(c * WIDE, (c + 1) * WIDE)
+            nc.vector.scalar_tensor_tensor(far[:, t, cols], gate[t][:, cols], 1.0, far[:, t, cols], ALU.add, ALU.mult)
+
+        def project_pair(pair, c):
+            bank = psum.tile([P, S], F32, name="bank")
+            for u in range(2):
+                product(bank[:, u * WIDE:(u + 1) * WIDE], w3_q, 2 * pair + u, z_q[c][0][:], z_q[c][1][:])
+            h = sb("h%d_%d" % (pair, c), [P, S], F32)
+            nc.scalar.copy(out=h[:], in_=bank[:])
+            return h
+
+        def difference(t):
+            fetch(gate[t][:], d_rows[t], n2_list)
+            nc.vector.tensor_tensor(gate[t][:], gate[t][:], d_banks[t][:], ALU.subtract)
+
+        def squash(t):
+            nc.scalar.activation(gate[t][:], gate[t][:], ACT.Tanh, scale=0.5)
+            nc.vector.scalar_tensor_tensor(near[:, t, :], gate[t][:], 1.0, y_rows[t][:], ALU.subtract, ALU.mult)
+
+        def project_into(t, c, dst):
+            bank = psum.tile([P, S], F32, name="bank")
+            for k in c:
+                product(bank[:, k * WIDE:(k + 1) * WIDE], w3_q, t, z_q[k][0][:], z_q[k][1][:])
+            nc.scalar.copy(out=dst, in_=bank[:, c[0] * WIDE:(c[-1] + 1) * WIDE])
+
+        on_vector = ()
+        w3_dealt = sb("w3_dealt", [P, PACK * N], BF16)
+        for t in range(PACK):
+            (nc.scalar.copy if t in (0,) else nc.vector.tensor_copy)(out=d_rows[t][:], in_=d_banks[t][:])
+        for t in range(PACK):
+            if t not in (3,):
+                leave_y(t)
+        for t in range(PACK):
+            difference(t)
+            if t in (1, 2):
+                deal_half(nc.vector.tensor_copy, w3_dealt, w3_raw[t - 1], t - 1)
+            if (t, 0) in on_vector:
+                fetch_half(far[:, t, :], y_rows[t], n1_list, 0, True)
+        for t in (3,):
+            leave_y(t)
+        w3_q = quantise("w3", w3_dealt[:], N)
+        z_q = []
+        for c in range(2):
+            for t in range(PACK):
+                if c == 0:
+                    squash(t)
+                if (t, c) not in on_vector:
+                    fetch_half(far[:, t, :], y_rows[t], n1_list, c, False)
+                weigh_far(t, c)
+                if c == 0 and (t, 1) in on_vector:
+                    fetch_half(far[:, t, :], y_rows[t], n1_list, 1, True)
+            z_q.append(quantise_z(c))
+        first = near[:, 0, WIDE:S]
+        project_into(0, (0,), first)
+        write_page(0, 0, first)
+        h = [sb("h%d" % t, [P, S], F32) for t in range(PACK)]
+        project_into(0, (1,), h[0][:, WIDE:S])
+        write_page(0, 1, h[0][:, WIDE:S])
+        for t in range(1, PACK):
+            project_into(t, (0, 1), h[t][:])
+            nc.vector.tensor_copy(page[t][:].indirect(n3_list[:]), h[t][:])
+        for t in range(PACK - 1):
+            for half in range(2):
+                read_page(t, half * HALF_U, HALF_U, False, True)
+        for quarter in range(4):
+            read_page(PACK - 1, quarter * WIDE, WIDE, quarter >= 2, True)

@@ -3,7 +3,7 @@ from contextlib import ExitStack
 import concourse.mybir as mybir
 
 K, T, S, N, H, U = 512, 2048, 512, 512, 512, 1024
-FLOPS = 3 * 2 * 512 * 512 * 512
+FLOPS = 2 * S * (2 * K * H + H * N)
 
 F32 = mybir.dt.float32
 BF16 = mybir.dt.bfloat16
@@ -17,10 +17,15 @@ ALU = mybir.AluOpType
 
 P = 128
 PACK = 4
-WIDE = 256
-SCALE_ROW0 = 14
+GROUP = 16
+QUADRANT = 32
+CHUNK = S // 2
+HALF_COLS = H // 2
+HALF_M = HALF_COLS // PACK
+SCALE_ROW0 = GROUP - 2
 SHIFT_ROWS = 112
-HALF_U = U // 2
+FETCH_BUFS = 3
+EARLY_TILE = 1
 
 
 def tile_picked_twhpullbpagem_none_p_kernel(tc, x_words, x_scales, w1, w2, gn, w3, mem, offs, hz, n1, n2, n3, n4, out):
@@ -29,8 +34,17 @@ def tile_picked_twhpullbpagem_none_p_kernel(tc, x_words, x_scales, w1, w2, gn, w
         keep = ctx.enter_context(tc.tile_pool(name="keep", bufs=1))
         psum = ctx.enter_context(tc.psum_pool(name="psum", bufs=8))
 
-        def sb(name, shape, dtype):
+        def sbuf(name, shape, dtype):
             return keep.tile(shape, dtype, name=name, align_bytes=64)
+
+        def bank():
+            return psum.tile([P, S], F32, name="bank")
+
+        def chunk(c):
+            return slice(c * CHUNK, (c + 1) * CHUNK)
+
+        def entries(lst, start, count):
+            return lst[:, start // GROUP:(start + count) // GROUP]
 
         def load_list(name, src):
             tile = keep.tile(list(src.shape), U16, name=name)
@@ -38,227 +52,179 @@ def tile_picked_twhpullbpagem_none_p_kernel(tc, x_words, x_scales, w1, w2, gn, w
             return tile
 
         def load_weight_half(name, w, half):
-            raw = sb(name, [P, PACK, H // 2], F32)
-            cols = slice(half * (H // 2), (half + 1) * (H // 2))
+            raw = sbuf(name, [P, PACK, HALF_COLS], F32)
+            cols = slice(half * HALF_COLS, (half + 1) * HALF_COLS)
             nc.sync.dma_start(out=raw[:], in_=w.rearrange("(p j) c -> p j c", j=PACK)[:, :, cols])
             return raw
 
-        def deal_half(copy, dealt, raw, half):
-            dst = dealt[:].rearrange("p (a e m j) -> p a m j e", a=2, e=2, j=PACK)[:, :, half * 64:(half + 1) * 64]
-            copy(out=dst, in_=raw[:].rearrange("p j (m a e) -> p a m j e", a=2, e=2))
+        def deal_by_pairs(copy, dealt, raw, half):
+            dst = dealt[:].rearrange("p (a e m j) -> p a m j e", a=2, e=2, j=PACK)
+            copy(out=dst[:, :, half * HALF_M:(half + 1) * HALF_M], in_=raw[:].rearrange("p j (m a e) -> p a m j e", a=2, e=2))
 
-        def quantise(name, src, width):
-            codes = sb(name + "_codes", [P, width], U32)
-            scales = sb(name + "_scales", [P, width], U8)
-            nc.vector.quantize_mx(out=codes[:].bitcast(FP8X4), scales=scales[:], in_=src)
+        def deal_on_gpsimd(dealt, raw, half):
+            dst = dealt[:].rearrange("p (t m j) -> p t m j", t=PACK, j=PACK)
+            nc.gpsimd.tensor_copy(out=dst[:, :, half * HALF_M:(half + 1) * HALF_M], in_=raw[:].rearrange("p j (m t) -> p t m j", t=PACK))
+
+        def quantise(name, values, width):
+            codes = sbuf(name + "_codes", [P, width], U32)
+            scales = sbuf(name + "_scales", [P, width], U8)
+            nc.vector.quantize_mx(out=codes[:].bitcast(FP8X4), scales=scales[:], in_=values[:])
             return codes, scales
 
-        def product(acc, weight, t, codes, scales):
+        def product(acc, weight, t, moving):
             cols = slice(t * P, (t + 1) * P)
             nc.tensor.matmul_mx(out=acc, lhsT=weight[0][:, cols].bitcast(FP8X4), lhsT_scale=weight[1][:, cols],
-                                rhs=codes.bitcast(FP8X4), rhs_scale=scales, start=True, stop=True)
+                                rhs=moving[0][:].bitcast(FP8X4), rhs_scale=moving[1][:], start=True, stop=True)
 
-        def piece(lst, start, count):
-            return lst[:, start // 16:(start + count) // 16]
-
-        x_bytes = sb("x_bytes", [P, T], U8)
-        d_plane = sb("d_plane", [P, S], U8)
-        y_plane = sb("y_plane", [P, S], U8)
+        x_bytes = sbuf("x_bytes", [P, T], U8)
+        d_scales = sbuf("d_scales", [P, S], U8)
+        y_scales = sbuf("y_scales", [P, S], U8)
         nc.vector.memset(x_bytes[:].bitcast(I32), 0)
-        nc.gpsimd.memset(d_plane[:].bitcast(I32), 0)
-        nc.gpsimd.memset(y_plane[:].bitcast(I32), 0)
+        nc.gpsimd.memset(d_scales[:].bitcast(I32), 0)
+        nc.gpsimd.memset(y_scales[:].bitcast(I32), 0)
 
         w2_raw = [load_weight_half("w2_raw0", w2, 0)]
-        for q in range(4):
-            row = 32 * q + SCALE_ROW0
-            nc.sync.dma_start(out=x_bytes[row:row + 4, :].bitcast(I32), in_=x_scales[0][4 * q:4 * q + 4, :].bitcast(I32))
+        for q in range(P // QUADRANT):
+            row = QUADRANT * q + SCALE_ROW0
+            nc.sync.dma_start(out=x_bytes[row:row + PACK, :].bitcast(I32), in_=x_scales[0][PACK * q:PACK * (q + 1), :].bitcast(I32))
         hz_list = load_list("hz_list", hz)
         offs_list = load_list("offs_list", offs)
-        x_codes = sb("x_codes", [P, T], U32)
+        x_codes = sbuf("x_codes", [P, T], U32)
         nc.sync.dma_start(out=x_codes[:].bitcast(I32), in_=x_words[0].rearrange("p n t -> p (n t)").bitcast(I32))
         w2_raw.append(load_weight_half("w2_raw1", w2, 1))
         w1_raw = [load_weight_half("w1_raw%d" % half, w1, half) for half in range(2)]
         n2_list = load_list("n2_list", n2)
-        gain = sb("gain", [P, PACK], F32)
+        gain = sbuf("gain", [P, PACK], F32)
         nc.sync.dma_start(out=gain[:], in_=gn.rearrange("(p t) o -> p (t o)", t=PACK))
         n1_list = load_list("n1_list", n1)
         w3_raw = [load_weight_half("w3_raw%d" % half, w3, half) for half in range(2)]
         n3_list = load_list("n3_list", n3)
         page = []
         for t in range(PACK):
-            tile = sb("page%d" % t, [P, U], F32)
-            nc.sync.dma_start(out=tile[:], in_=mem.rearrange("(p t) w -> t p w", t=PACK)[t])
-            page.append(tile)
+            page.append(sbuf("page%d" % t, [P, U], F32))
+            nc.sync.dma_start(out=page[t][:], in_=mem.rearrange("(p t) w -> t p w", t=PACK)[t])
         n4_list = load_list("n4_list", n4)
 
-        def gather_bytes(name, lst, plane):
-            picked = sb(name, [P, S], U8)
+        def gather_scales(name, lst, scales):
+            picked = sbuf(name, [P, S], U8)
             nc.vector.tensor_copy(picked[:], x_bytes[:].indirect(lst[:]))
-            nc.scalar.dma_start(out=plane[0:SHIFT_ROWS, :].bitcast(I32),
+            nc.scalar.dma_start(out=scales[0:SHIFT_ROWS, :].bitcast(I32),
                                 in_=picked[SCALE_ROW0:SCALE_ROW0 + SHIFT_ROWS, :].bitcast(I32))
 
         def gather_words(name, lst):
-            picked = sb(name, [P, S], U32)
+            picked = sbuf(name, [P, S], U32)
             nc.vector.tensor_copy(picked[:], x_codes[:].indirect(lst[:]))
             return picked
 
-        def first_product(weight, words, plane):
+        def four_tiles(weight, moving):
             banks = []
             for t in range(PACK):
-                bank = psum.tile([P, S], F32, name="bank")
-                product(bank[:], weight, t, words[:], plane[:])
-                banks.append(bank)
+                banks.append(bank())
+                product(banks[t][:], weight, t, moving)
             return banks
 
-        gather_bytes("hz_bytes", hz_list, d_plane)
-        gather_bytes("offs_bytes", offs_list, y_plane)
+        gather_scales("hz_bytes", hz_list, d_scales)
+        gather_scales("offs_bytes", offs_list, y_scales)
         hz_words = gather_words("hz_words", hz_list)
-        w2_dealt = sb("w2_dealt", [P, PACK * H], BF16)
-        deal_half(nc.scalar.copy, w2_dealt, w2_raw[0], 0)
-        deal_half(nc.scalar.copy, w2_dealt, w2_raw[1], 1)
-        d_banks = first_product(quantise("w2", w2_dealt[:], H), hz_words, d_plane)
+        w2_dealt = sbuf("w2_dealt", [P, PACK * H], BF16)
+        for half in range(2):
+            deal_by_pairs(nc.scalar.copy, w2_dealt, w2_raw[half], half)
+        d_banks = four_tiles(quantise("w2", w2_dealt, H), (hz_words, d_scales))
         offs_words = gather_words("offs_words", offs_list)
-        w1_dealt = sb("w1_dealt", [P, PACK * H], BF16)
-        deal_half(nc.scalar.copy, w1_dealt, w1_raw[0], 0)
-        deal_half(nc.vector.tensor_copy, w1_dealt, w1_raw[1], 1)
-        y_banks = first_product(quantise("w1", w1_dealt[:], H), offs_words, y_plane)
-        half_gain = sb("half_gain", [P, PACK], F32)
+        w1_dealt = sbuf("dealt", [P, PACK * H], BF16)
+        deal_by_pairs(nc.scalar.copy, w1_dealt, w1_raw[0], 0)
+        deal_by_pairs(nc.vector.tensor_copy, w1_dealt, w1_raw[1], 1)
+        y_banks = four_tiles(quantise("w1", w1_dealt, H), (offs_words, y_scales))
+        half_gain = sbuf("half_gain", [P, PACK], F32)
         nc.scalar.activation(half_gain[:], gain[:], ACT.Copy, scale=0.5)
 
-        d_rows = [sb("d%d" % t, [P, S], F32) for t in range(PACK)]
-        y_rows = [sb("y%d" % t, [P, S], F32) for t in range(PACK)]
-        gate = [sb("gate%d" % t, [P, S], F32) for t in range(PACK)]
-        far = sb("far", [P, PACK, S], F32)
-        near = sb("near", [P, PACK, S], F32)
-
-        def fetch(dst, rows, lst, on_vector=False):
-            for c in range(2):
-                looked_up = rows[:].indirect(piece(lst, c * WIDE, WIDE))
-                if on_vector:
-                    nc.vector.tensor_copy(dst[:, c * WIDE:(c + 1) * WIDE], looked_up)
-                else:
-                    nc.scalar.activation(dst[:, c * WIDE:(c + 1) * WIDE], looked_up, ACT.Copy)
-
-        def gate_tile(t):
-            nc.scalar.copy(out=d_rows[t][:], in_=d_banks[t][:])
-            fetch(gate[t][:], d_rows[t], n2_list)
-            nc.vector.tensor_tensor(gate[t][:], gate[t][:], d_rows[t][:], ALU.subtract)
-            nc.scalar.activation(gate[t][:], gate[t][:], ACT.Tanh, scale=0.5)
-
-        def mix_tile(t):
-            if t in (3,):
-                nc.scalar.activation(y_rows[t][:], y_banks[t][:], ACT.Copy, scale=half_gain[:, t:t + 1])
-            else:
-                nc.vector.tensor_scalar(y_rows[t][:], y_banks[t][:], half_gain[:, t:t + 1], None, ALU.mult)
-            fetch(far[:, t, :], y_rows[t], n1_list, t in ())
-            nc.vector.scalar_tensor_tensor(near[:, t, :], gate[t][:], 1.0, y_rows[t][:], ALU.subtract, ALU.mult)
-            nc.vector.scalar_tensor_tensor(far[:, t, :], gate[t][:], 1.0, far[:, t, :], ALU.add, ALU.mult)
-
-        def quantise_z(c):
-            cols = slice(c * WIDE, (c + 1) * WIDE)
-            z = sb("z%d" % c, [P, PACK * WIDE], BF16)
-            nc.vector.tensor_tensor(z[:].rearrange("p (c e t) -> p c t e", e=2, t=PACK),
-                                    far[:, :, cols].rearrange("p t (c e) -> p c t e", e=2),
-                                    near[:, :, cols].rearrange("p t (c e) -> p c t e", e=2), ALU.subtract)
-            return quantise("z%d" % c, z[:], WIDE)
-
-        def project(t, z_q, c, h):
-            bank = psum.tile([P, S], F32, name="bank")
-            product(bank[:, 0:WIDE], w3_q, t, z_q[0][:], z_q[1][:])
-            nc.scalar.copy(out=h, in_=bank[:, 0:WIDE])
-
-        def write_page(t, c, h):
-            nc.vector.tensor_copy(page[t][:].indirect(piece(n3_list, c * WIDE, WIDE)), h)
-
-        def read_page(t, w0, n, fetch_on_vector, add_on_gpsimd):
-            res = sb("res%d_%d" % (t, w0), [P, n], F32)
-            looked_up = page[t][:].indirect(piece(n4_list, w0, n))
-            own = page[t][:, w0:w0 + n]
-            if fetch_on_vector:
-                nc.vector.tensor_copy(res[:], looked_up)
-                nc.vector.scalar_tensor_tensor(res[:], res[:], -0.5, own, ALU.mult, ALU.add)
-            else:
-                nc.scalar.activation(res[:], looked_up, ACT.Copy, scale=-0.5)
-                (nc.gpsimd if add_on_gpsimd else nc.vector).tensor_tensor(res[:], res[:], own, ALU.add)
-            (nc.scalar if fetch_on_vector else nc.sync).dma_start(out=out.rearrange("(p t) w -> t p w", t=PACK)[t][:, w0:w0 + n], in_=res[:])
-
-        def leave_y(t):
-            if t in (3,):
-                nc.scalar.activation(y_rows[t][:], y_banks[t][:], ACT.Copy, scale=half_gain[:, t:t + 1])
-            else:
-                nc.vector.tensor_scalar(y_rows[t][:], y_banks[t][:], half_gain[:, t:t + 1], None, ALU.mult)
-
-        def fetch_half(dst, rows, lst, c, on_vector):
-            looked_up = rows[:].indirect(piece(lst, c * WIDE, WIDE))
-            if on_vector:
-                nc.vector.tensor_copy(dst[:, c * WIDE:(c + 1) * WIDE], looked_up)
-            else:
-                nc.scalar.activation(dst[:, c * WIDE:(c + 1) * WIDE], looked_up, ACT.Copy)
-
-        def weigh_far(t, c):
-            cols = slice(c * WIDE, (c + 1) * WIDE)
-            nc.vector.scalar_tensor_tensor(far[:, t, cols], gate[t][:, cols], 1.0, far[:, t, cols], ALU.add, ALU.mult)
-
-        def project_pair(pair, c):
-            bank = psum.tile([P, S], F32, name="bank")
-            for u in range(2):
-                product(bank[:, u * WIDE:(u + 1) * WIDE], w3_q, 2 * pair + u, z_q[c][0][:], z_q[c][1][:])
-            h = sb("h%d_%d" % (pair, c), [P, S], F32)
-            nc.scalar.copy(out=h[:], in_=bank[:])
-            return h
+        d_rows = [sbuf("d%d" % t, [P, S], F32) for t in range(PACK)]
+        a_rows = [sbuf("a%d" % t, [P, S], F32) for t in range(PACK)]
+        gate = [sbuf("gate%d" % t, [P, S], F32) for t in range(PACK)]
+        far = sbuf("far", [P, 2, PACK, CHUNK], F32)
+        near = sbuf("near", [P, 2, PACK, CHUNK], F32)
 
         def difference(t):
-            fetch(gate[t][:], d_rows[t], n2_list)
+            for c in range(2):
+                nc.scalar.activation(gate[t][:, chunk(c)], d_rows[t][:].indirect(entries(n2_list, c * CHUNK, CHUNK)), ACT.Copy)
             nc.vector.tensor_tensor(gate[t][:], gate[t][:], d_banks[t][:], ALU.subtract)
 
-        def squash(t):
+        def weigh_near(t):
             nc.scalar.activation(gate[t][:], gate[t][:], ACT.Tanh, scale=0.5)
-            nc.vector.scalar_tensor_tensor(near[:, t, :], gate[t][:], 1.0, y_rows[t][:], ALU.subtract, ALU.mult)
+            nc.vector.scalar_tensor_tensor(near[:, :, t, :], gate[t][:].rearrange("p (c w) -> p c w", c=2), 1.0,
+                                           a_rows[t][:].rearrange("p (c w) -> p c w", c=2), ALU.subtract, ALU.mult)
 
-        def project_into(t, c, dst):
-            bank = psum.tile([P, S], F32, name="bank")
-            for k in c:
-                product(bank[:, k * WIDE:(k + 1) * WIDE], w3_q, t, z_q[k][0][:], z_q[k][1][:])
-            nc.scalar.copy(out=dst, in_=bank[:, c[0] * WIDE:(c[-1] + 1) * WIDE])
+        def weigh_far(t, c):
+            fetched = keep.tile([P, CHUNK], F32, name="fetched", bufs=FETCH_BUFS, align_bytes=64)
+            nc.scalar.activation(fetched[:], a_rows[t][:].indirect(entries(n1_list, c * CHUNK, CHUNK)), ACT.Copy)
+            nc.vector.scalar_tensor_tensor(far[:, c, t, :], gate[t][:, chunk(c)], 1.0, fetched[:], ALU.add, ALU.mult)
 
-        on_vector = ()
-        w3_dealt = sb("w3_dealt", [P, PACK * N], BF16)
-        for t in range(PACK):
-            (nc.scalar.copy if t in (0,) else nc.vector.tensor_copy)(out=d_rows[t][:], in_=d_banks[t][:])
-        for t in range(PACK):
-            if t not in (3,):
-                leave_y(t)
+        def make_z(c):
+            z = sbuf("z%d" % c, [P, PACK * CHUNK], BF16)
+            nc.vector.tensor_tensor(z[:].rearrange("p (v e t) -> p v t e", e=2, t=PACK),
+                                    far[:, c].rearrange("p t (v e) -> p v t e", e=2),
+                                    near[:, c].rearrange("p t (v e) -> p v t e", e=2), ALU.subtract)
+            return z
+
+        w3_dealt = sbuf("dealt", [P, PACK * N], BF16)
+        nc.scalar.copy(out=d_rows[0][:], in_=d_banks[0][:])
+        for t in range(1, PACK):
+            nc.vector.tensor_copy(out=d_rows[t][:], in_=d_banks[t][:])
         for t in range(PACK):
             difference(t)
-            if t in (1, 2):
-                deal_half(nc.vector.tensor_copy, w3_dealt, w3_raw[t - 1], t - 1)
-            if (t, 0) in on_vector:
-                fetch_half(far[:, t, :], y_rows[t], n1_list, 0, True)
-        for t in (3,):
-            leave_y(t)
-        w3_q = quantise("w3", w3_dealt[:], N)
-        z_q = []
-        for c in range(2):
-            for t in range(PACK):
-                if c == 0:
-                    squash(t)
-                if (t, c) not in on_vector:
-                    fetch_half(far[:, t, :], y_rows[t], n1_list, c, False)
-                weigh_far(t, c)
-                if c == 0 and (t, 1) in on_vector:
-                    fetch_half(far[:, t, :], y_rows[t], n1_list, 1, True)
-            z_q.append(quantise_z(c))
-        first = near[:, 0, WIDE:S]
-        project_into(0, (0,), first)
-        write_page(0, 0, first)
-        h = [sb("h%d" % t, [P, S], F32) for t in range(PACK)]
-        project_into(0, (1,), h[0][:, WIDE:S])
-        write_page(0, 1, h[0][:, WIDE:S])
-        for t in range(1, PACK):
-            project_into(t, (0, 1), h[t][:])
-            nc.vector.tensor_copy(page[t][:].indirect(n3_list[:]), h[t][:])
+            nc.vector.tensor_scalar(a_rows[t][:], y_banks[t][:], half_gain[:, t:t + 1], None, ALU.mult)
+        for half in range(2):
+            deal_on_gpsimd(w3_dealt, w3_raw[half], half)
+        w3_q = quantise("w3", w3_dealt, N)
+        for t in range(PACK):
+            weigh_near(t)
+            weigh_far(t, 0)
+        z_first = make_z(0)
+        for t in range(PACK):
+            weigh_far(t, 1)
+        z_q = [quantise("z0", z_first, CHUNK)]
+        z_q.append(quantise("z1", make_z(1), CHUNK))
+
+        def project(t, chunks, dst):
+            acc = bank()
+            for c in chunks:
+                product(acc[:, chunk(c)], w3_q, t, z_q[c])
+            nc.scalar.copy(out=dst, in_=acc[:, chunks[0] * CHUNK:(chunks[-1] + 1) * CHUNK])
+
+        def write_page(t, start, count, src):
+            nc.vector.tensor_copy(page[t][:].indirect(entries(n3_list, start, count)), src)
+
+        early = near[:, 1, 0, :]
+        project(EARLY_TILE, (0,), early)
+        write_page(EARLY_TILE, 0, CHUNK, early)
+        for t in range(PACK):
+            chunks = (1,) if t == EARLY_TILE else (0, 1)
+            start = chunks[0] * CHUNK
+            h = sbuf("h%d" % t, [P, S], F32)
+            project(t, chunks, h[:, start:S])
+            write_page(t, start, S - start, h[:, start:S])
+
+        out_tiles = out.rearrange("(p t) w -> t p w", t=PACK)
+
+        def fetch_on_scalar(t, start, count):
+            res = sbuf("res%d_%d" % (t, start), [P, count], F32)
+            nc.scalar.activation(res[:], page[t][:].indirect(entries(n4_list, start, count)), ACT.Copy, scale=-0.5)
+            return res
+
         for t in range(PACK - 1):
-            for half in range(2):
-                read_page(t, half * HALF_U, HALF_U, False, True)
-        for quarter in range(4):
-            read_page(PACK - 1, quarter * WIDE, WIDE, quarter >= 2, True)
+            for start in range(0, U, U // 2):
+                slots = slice(start, start + U // 2)
+                res = fetch_on_scalar(t, start, U // 2)
+                nc.gpsimd.tensor_tensor(res[:], res[:], page[t][:, slots], ALU.add)
+                nc.sync.dma_start(out=out_tiles[t][:, slots], in_=res[:])
+        last = PACK - 1
+        for start in range(0, U, U // 4):
+            slots = slice(start, start + U // 4)
+            if start < U // 2:
+                res = fetch_on_scalar(last, start, U // 4)
+                nc.vector.tensor_tensor(res[:], res[:], page[last][:, slots], ALU.add)
+            else:
+                res = sbuf("res%d_%d" % (last, start), [P, U // 4], F32)
+                nc.vector.tensor_copy(res[:], page[last][:].indirect(entries(n4_list, start, U // 4)))
+                nc.vector.scalar_tensor_tensor(res[:], res[:], -0.5, page[last][:, slots], ALU.mult, ALU.add)
+            nc.scalar.dma_start(out=out_tiles[last][:, slots], in_=res[:])

@@ -24,6 +24,8 @@ HALF_COLS = H // 2
 HALF_M = HALF_COLS // PACK
 SCALE_ROW0 = GROUP - 2
 SHIFT_ROWS = 112
+RAW_SHAPE = [P, PACK, HALF_COLS]
+ROW_BYTES = 4 * S
 FETCH_BUFS = 3
 EARLY_TILE = 1
 
@@ -32,6 +34,7 @@ def tile_picked_twhpullbpagem_none_p_kernel(tc, x_words, x_scales, w1, w2, gn, w
     nc = tc.nc
     with ExitStack() as ctx:
         keep = ctx.enter_context(tc.tile_pool(name="keep", bufs=1))
+        shared = ctx.enter_context(tc.tile_pool(name="shared", bufs=1))
         psum = ctx.enter_context(tc.psum_pool(name="psum", bufs=8))
 
         def sbuf(name, shape, dtype):
@@ -51,15 +54,14 @@ def tile_picked_twhpullbpagem_none_p_kernel(tc, x_words, x_scales, w1, w2, gn, w
             nc.sync.dma_start(tile[:], src)
             return tile
 
-        def load_weight_half(name, w, half):
-            raw = sbuf(name, [P, PACK, HALF_COLS], F32)
+        def load_weight_half(raw, w, half):
             cols = slice(half * HALF_COLS, (half + 1) * HALF_COLS)
             nc.sync.dma_start(out=raw[:], in_=w.rearrange("(p j) c -> p j c", j=PACK)[:, :, cols])
             return raw
 
         def deal_by_pairs(copy, dealt, raw, half):
-            dst = dealt[:].rearrange("p (a e m j) -> p a m j e", a=2, e=2, j=PACK)
-            copy(out=dst[:, :, half * HALF_M:(half + 1) * HALF_M], in_=raw[:].rearrange("p j (m a e) -> p a m j e", a=2, e=2))
+            dst = dealt[:].rearrange("p (u e m j) -> p u m j e", u=2, e=2, j=PACK)
+            copy(out=dst[:, :, half * HALF_M:(half + 1) * HALF_M], in_=raw[:].rearrange("p j (m u e) -> p u m j e", u=2, e=2))
 
         def deal_on_gpsimd(dealt, raw, half):
             dst = dealt[:].rearrange("p (t m j) -> p t m j", t=PACK, j=PACK)
@@ -69,6 +71,15 @@ def tile_picked_twhpullbpagem_none_p_kernel(tc, x_words, x_scales, w1, w2, gn, w
             codes = sbuf(name + "_codes", [P, width], U32)
             scales = sbuf(name + "_scales", [P, width], U8)
             nc.vector.quantize_mx(out=codes[:].bitcast(FP8X4), scales=scales[:], in_=values[:])
+            return codes, scales
+
+        def quantise_in_two(name, values, width):
+            codes = sbuf(name + "_codes", [P, width], U32)
+            scales = sbuf(name + "_scales", [P, width], U8)
+            for part in range(2):
+                start, stop = part * width // 2, (part + 1) * width // 2
+                nc.vector.quantize_mx(out=codes[:, start:stop].bitcast(FP8X4), scales=scales[:, start:stop],
+                                      in_=values[:, PACK * start:PACK * stop])
             return codes, scales
 
         def product(acc, weight, t, moving):
@@ -83,7 +94,7 @@ def tile_picked_twhpullbpagem_none_p_kernel(tc, x_words, x_scales, w1, w2, gn, w
         nc.gpsimd.memset(d_scales[:].bitcast(I32), 0)
         nc.gpsimd.memset(y_scales[:].bitcast(I32), 0)
 
-        w2_raw = [load_weight_half("w2_raw0", w2, 0)]
+        w2_raw = [load_weight_half(sbuf("w2_raw0", RAW_SHAPE, F32), w2, 0)]
         for q in range(P // QUADRANT):
             row = QUADRANT * q + SCALE_ROW0
             nc.sync.dma_start(out=x_bytes[row:row + PACK, :].bitcast(I32), in_=x_scales[0][PACK * q:PACK * (q + 1), :].bitcast(I32))
@@ -91,13 +102,14 @@ def tile_picked_twhpullbpagem_none_p_kernel(tc, x_words, x_scales, w1, w2, gn, w
         offs_list = load_list("offs_list", offs)
         x_codes = sbuf("x_codes", [P, T], U32)
         nc.sync.dma_start(out=x_codes[:].bitcast(I32), in_=x_words[0].rearrange("p n t -> p (n t)").bitcast(I32))
-        w2_raw.append(load_weight_half("w2_raw1", w2, 1))
-        w1_raw = [load_weight_half("w1_raw%d" % half, w1, half) for half in range(2)]
+        w2_raw.append(load_weight_half(sbuf("w2_raw1", RAW_SHAPE, F32), w2, 1))
+        w1_raw = [load_weight_half(sbuf("w1_raw0", RAW_SHAPE, F32), w1, 0),
+                  load_weight_half(shared.tile(RAW_SHAPE, F32, name="w1_raw1", offset=ROW_BYTES // 2), w1, 1)]
         n2_list = load_list("n2_list", n2)
         gain = sbuf("gain", [P, PACK], F32)
         nc.sync.dma_start(out=gain[:], in_=gn.rearrange("(p t) o -> p (t o)", t=PACK))
         n1_list = load_list("n1_list", n1)
-        w3_raw = [load_weight_half("w3_raw%d" % half, w3, half) for half in range(2)]
+        w3_raw = [load_weight_half(sbuf("w3_raw%d" % half, RAW_SHAPE, F32), w3, half) for half in range(2)]
         n3_list = load_list("n3_list", n3)
         page = []
         for t in range(PACK):
@@ -105,11 +117,16 @@ def tile_picked_twhpullbpagem_none_p_kernel(tc, x_words, x_scales, w1, w2, gn, w
             nc.sync.dma_start(out=page[t][:], in_=mem.rearrange("(p t) w -> t p w", t=PACK)[t])
         n4_list = load_list("n4_list", n4)
 
-        def gather_scales(name, lst, scales):
+        def gather_scales(name, lst, scales, by_quadrant):
             picked = sbuf(name, [P, S], U8)
             nc.vector.tensor_copy(picked[:], x_bytes[:].indirect(lst[:]))
-            nc.scalar.dma_start(out=scales[0:SHIFT_ROWS, :].bitcast(I32),
-                                in_=picked[SCALE_ROW0:SCALE_ROW0 + SHIFT_ROWS, :].bitcast(I32))
+            if by_quadrant:
+                for row in range(0, P, QUADRANT):
+                    nc.scalar.dma_start(out=scales[row:row + PACK, :].bitcast(I32),
+                                        in_=picked[row + SCALE_ROW0:row + SCALE_ROW0 + PACK, :].bitcast(I32))
+            else:
+                nc.scalar.dma_start(out=scales[0:SHIFT_ROWS, :].bitcast(I32),
+                                    in_=picked[SCALE_ROW0:SCALE_ROW0 + SHIFT_ROWS, :].bitcast(I32))
 
         def gather_words(name, lst):
             picked = sbuf(name, [P, S], U32)
@@ -123,13 +140,13 @@ def tile_picked_twhpullbpagem_none_p_kernel(tc, x_words, x_scales, w1, w2, gn, w
                 product(banks[t][:], weight, t, moving)
             return banks
 
-        gather_scales("hz_bytes", hz_list, d_scales)
-        gather_scales("offs_bytes", offs_list, y_scales)
+        gather_scales("hz_bytes", hz_list, d_scales, by_quadrant=True)
+        gather_scales("offs_bytes", offs_list, y_scales, by_quadrant=False)
         hz_words = gather_words("hz_words", hz_list)
         w2_dealt = sbuf("w2_dealt", [P, PACK * H], BF16)
         for half in range(2):
             deal_by_pairs(nc.scalar.copy, w2_dealt, w2_raw[half], half)
-        d_banks = four_tiles(quantise("w2", w2_dealt, H), (hz_words, d_scales))
+        d_banks = four_tiles(quantise_in_two("w2", w2_dealt, H), (hz_words, d_scales))
         offs_words = gather_words("offs_words", offs_list)
         w1_dealt = sbuf("dealt", [P, PACK * H], BF16)
         deal_by_pairs(nc.scalar.copy, w1_dealt, w1_raw[0], 0)
@@ -138,7 +155,8 @@ def tile_picked_twhpullbpagem_none_p_kernel(tc, x_words, x_scales, w1, w2, gn, w
         half_gain = sbuf("half_gain", [P, PACK], F32)
         nc.scalar.activation(half_gain[:], gain[:], ACT.Copy, scale=0.5)
 
-        d_rows = [sbuf("d%d" % t, [P, S], F32) for t in range(PACK)]
+        d_rows = [sbuf("d0", [P, S], F32)]
+        d_rows.extend(shared.tile([P, S], F32, name="d%d" % t, offset=(t - 1) * ROW_BYTES) for t in range(1, PACK))
         a_rows = [sbuf("a%d" % t, [P, S], F32) for t in range(PACK)]
         gate = [sbuf("gate%d" % t, [P, S], F32) for t in range(PACK)]
         far = sbuf("far", [P, 2, PACK, CHUNK], F32)

from contextlib import ExitStack

import concourse.mybir as mybir

K, T, S, N, H, U = 512, 2048, 512, 512, 512, 1024
FLOPS = 2 * S * (2 * K * H + H * N)

F32 = mybir.dt.float32
BF16 = mybir.dt.bfloat16
I32 = mybir.dt.int32
U32 = mybir.dt.uint32
U16 = mybir.dt.uint16
U8 = mybir.dt.uint8
FP8X4 = mybir.dt.float8_e4m3fn_x4
ACT = mybir.ActivationFunctionType
ALU = mybir.AluOpType

P = 128
PACK = 4
GROUP = 16
QUADRANT = 32
CHUNK = S // 2
HALF_COLS = H // 2
HALF_M = HALF_COLS // PACK
SCALE_ROW0 = GROUP - 2
SHIFT_ROWS = 112
RAW_SHAPE = [P, PACK, HALF_COLS]
ROW_BYTES = 4 * S
FETCH_BUFS = 3
EARLY_TILE = 1


def tile_picked_twhpullbpagem_none_p_kernel(tc, x_words, x_scales, w1, w2, gn, w3, mem, offs, hz, n1, n2, n3, n4, out):
    nc = tc.nc
    with ExitStack() as ctx:
        keep = ctx.enter_context(tc.tile_pool(name="keep", bufs=1))
        shared = ctx.enter_context(tc.tile_pool(name="shared", bufs=1))
        psum = ctx.enter_context(tc.psum_pool(name="psum", bufs=8))

        def sbuf(name, shape, dtype):
            return keep.tile(shape, dtype, name=name, align_bytes=64)

        def bank():
            return psum.tile([P, S], F32, name="bank")

        def chunk(c):
            return slice(c * CHUNK, (c + 1) * CHUNK)

        def entries(lst, start, count):
            return lst[:, start // GROUP:(start + count) // GROUP]

        def load_list(name, src):
            tile = keep.tile(list(src.shape), U16, name=name)
            nc.sync.dma_start(tile[:], src)
            return tile

        def load_weight_half(raw, w, half):
            cols = slice(half * HALF_COLS, (half + 1) * HALF_COLS)
            nc.sync.dma_start(out=raw[:], in_=w.rearrange("(p j) c -> p j c", j=PACK)[:, :, cols])
            return raw

        def deal_by_pairs(copy, dealt, raw, half):
            dst = dealt[:].rearrange("p (u e m j) -> p u m j e", u=2, e=2, j=PACK)
            copy(out=dst[:, :, half * HALF_M:(half + 1) * HALF_M], in_=raw[:].rearrange("p j (m u e) -> p u m j e", u=2, e=2))

        def deal_on_gpsimd(dealt, raw, half):
            dst = dealt[:].rearrange("p (t m j) -> p t m j", t=PACK, j=PACK)
            nc.gpsimd.tensor_copy(out=dst[:, :, half * HALF_M:(half + 1) * HALF_M], in_=raw[:].rearrange("p j (m t) -> p t m j", t=PACK))

        def quantise(name, values, width):
            codes = sbuf(name + "_codes", [P, width], U32)
            scales = sbuf(name + "_scales", [P, width], U8)
            nc.vector.quantize_mx(out=codes[:].bitcast(FP8X4), scales=scales[:], in_=values[:])
            return codes, scales

        def quantise_in_two(name, values, width):
            codes = sbuf(name + "_codes", [P, width], U32)
            scales = sbuf(name + "_scales", [P, width], U8)
            for part in range(2):
                start, stop = part * width // 2, (part + 1) * width // 2
                nc.vector.quantize_mx(out=codes[:, start:stop].bitcast(FP8X4), scales=scales[:, start:stop],
                                      in_=values[:, PACK * start:PACK * stop])
            return codes, scales

        def product(acc, weight, t, moving):
            cols = slice(t * P, (t + 1) * P)
            nc.tensor.matmul_mx(out=acc, lhsT=weight[0][:, cols].bitcast(FP8X4), lhsT_scale=weight[1][:, cols],
                                rhs=moving[0][:].bitcast(FP8X4), rhs_scale=moving[1][:], start=True, stop=True)

        x_bytes = sbuf("x_bytes", [P, T], U8)
        d_scales = sbuf("d_scales", [P, S], U8)
        y_scales = sbuf("y_scales", [P, S], U8)
        nc.vector.memset(x_bytes[:].bitcast(I32), 0)
        nc.gpsimd.memset(d_scales[:].bitcast(I32), 0)
        nc.gpsimd.memset(y_scales[:].bitcast(I32), 0)

        w2_raw = [load_weight_half(sbuf("w2_raw0", RAW_SHAPE, F32), w2, 0)]
        for q in range(P // QUADRANT):
            row = QUADRANT * q + SCALE_ROW0
            nc.sync.dma_start(out=x_bytes[row:row + PACK, :].bitcast(I32), in_=x_scales[0][PACK * q:PACK * (q + 1), :].bitcast(I32))
        hz_list = load_list("hz_list", hz)
        offs_list = load_list("offs_list", offs)
        x_codes = sbuf("x_codes", [P, T], U32)
        nc.sync.dma_start(out=x_codes[:].bitcast(I32), in_=x_words[0].rearrange("p n t -> p (n t)").bitcast(I32))
        w2_raw.append(load_weight_half(sbuf("w2_raw1", RAW_SHAPE, F32), w2, 1))
        w1_raw = [load_weight_half(sbuf("w1_raw0", RAW_SHAPE, F32), w1, 0),
                  load_weight_half(shared.tile(RAW_SHAPE, F32, name="w1_raw1", offset=ROW_BYTES // 2), w1, 1)]
        n2_list = load_list("n2_list", n2)
        gain = sbuf("gain", [P, PACK], F32)
        nc.sync.dma_start(out=gain[:], in_=gn.rearrange("(p t) o -> p (t o)", t=PACK))
        n1_list = load_list("n1_list", n1)
        w3_raw = [load_weight_half(sbuf("w3_raw%d" % half, RAW_SHAPE, F32), w3, half) for half in range(2)]
        n3_list = load_list("n3_list", n3)
        page = []
        for t in range(PACK):
            page.append(sbuf("page%d" % t, [P, U], F32))
            nc.sync.dma_start(out=page[t][:], in_=mem.rearrange("(p t) w -> t p w", t=PACK)[t])
        n4_list = load_list("n4_list", n4)

        def gather_scales(name, lst, scales, by_quadrant):
            picked = sbuf(name, [P, S], U8)
            nc.vector.tensor_copy(picked[:], x_bytes[:].indirect(lst[:]))
            if by_quadrant:
                for row in range(0, P, QUADRANT):
                    nc.scalar.dma_start(out=scales[row:row + PACK, :].bitcast(I32),
                                        in_=picked[row + SCALE_ROW0:row + SCALE_ROW0 + PACK, :].bitcast(I32))
            else:
                nc.scalar.dma_start(out=scales[0:SHIFT_ROWS, :].bitcast(I32),
                                    in_=picked[SCALE_ROW0:SCALE_ROW0 + SHIFT_ROWS, :].bitcast(I32))

        def gather_words(name, lst):
            picked = sbuf(name, [P, S], U32)
            nc.vector.tensor_copy(picked[:], x_codes[:].indirect(lst[:]))
            return picked

        def four_tiles(weight, moving):
            banks = []
            for t in range(PACK):
                banks.append(bank())
                product(banks[t][:], weight, t, moving)
            return banks

        gather_scales("hz_bytes", hz_list, d_scales, by_quadrant=True)
        gather_scales("offs_bytes", offs_list, y_scales, by_quadrant=False)
        hz_words = gather_words("hz_words", hz_list)
        w2_dealt = sbuf("w2_dealt", [P, PACK * H], BF16)
        for half in range(2):
            deal_by_pairs(nc.scalar.copy, w2_dealt, w2_raw[half], half)
        d_banks = four_tiles(quantise_in_two("w2", w2_dealt, H), (hz_words, d_scales))
        offs_words = gather_words("offs_words", offs_list)
        w1_dealt = sbuf("dealt", [P, PACK * H], BF16)
        deal_by_pairs(nc.scalar.copy, w1_dealt, w1_raw[0], 0)
        deal_by_pairs(nc.vector.tensor_copy, w1_dealt, w1_raw[1], 1)
        y_banks = four_tiles(quantise("w1", w1_dealt, H), (offs_words, y_scales))
        half_gain = sbuf("half_gain", [P, PACK], F32)
        nc.scalar.activation(half_gain[:], gain[:], ACT.Copy, scale=0.5)

        d_rows = [sbuf("d0", [P, S], F32)]
        d_rows.extend(shared.tile([P, S], F32, name="d%d" % t, offset=(t - 1) * ROW_BYTES) for t in range(1, PACK))
        a_rows = [sbuf("a%d" % t, [P, S], F32) for t in range(PACK)]
        gate = [sbuf("gate%d" % t, [P, S], F32) for t in range(PACK)]
        far = sbuf("far", [P, 2, PACK, CHUNK], F32)
        near = sbuf("near", [P, 2, PACK, CHUNK], F32)

        def difference(t):
            for c in range(2):
                nc.scalar.activation(gate[t][:, chunk(c)], d_rows[t][:].indirect(entries(n2_list, c * CHUNK, CHUNK)), ACT.Copy)
            nc.vector.tensor_tensor(gate[t][:], gate[t][:], d_banks[t][:], ALU.subtract)

        def weigh_near(t):
            nc.scalar.activation(gate[t][:], gate[t][:], ACT.Tanh, scale=0.5)
            nc.vector.scalar_tensor_tensor(near[:, :, t, :], gate[t][:].rearrange("p (c w) -> p c w", c=2), 1.0,
                                           a_rows[t][:].rearrange("p (c w) -> p c w", c=2), ALU.subtract, ALU.mult)

        def weigh_far(t, c):
            fetched = keep.tile([P, CHUNK], F32, name="fetched", bufs=FETCH_BUFS, align_bytes=64)
            nc.scalar.activation(fetched[:], a_rows[t][:].indirect(entries(n1_list, c * CHUNK, CHUNK)), ACT.Copy)
            nc.vector.scalar_tensor_tensor(far[:, c, t, :], gate[t][:, chunk(c)], 1.0, fetched[:], ALU.add, ALU.mult)

        def make_z(c):
            z = sbuf("z%d" % c, [P, PACK * CHUNK], BF16)
            nc.vector.tensor_tensor(z[:].rearrange("p (v e t) -> p v t e", e=2, t=PACK),
                                    far[:, c].rearrange("p t (v e) -> p v t e", e=2),
                                    near[:, c].rearrange("p t (v e) -> p v t e", e=2), ALU.subtract)
            return z

        w3_dealt = sbuf("dealt", [P, PACK * N], BF16)
        nc.scalar.copy(out=d_rows[0][:], in_=d_banks[0][:])
        for t in range(1, PACK):
            nc.vector.tensor_copy(out=d_rows[t][:], in_=d_banks[t][:])
        for t in range(PACK):
            difference(t)
            nc.vector.tensor_scalar(a_rows[t][:], y_banks[t][:], half_gain[:, t:t + 1], None, ALU.mult)
        for half in range(2):
            deal_on_gpsimd(w3_dealt, w3_raw[half], half)
        w3_q = quantise("w3", w3_dealt, N)
        for t in range(PACK):
            weigh_near(t)
            weigh_far(t, 0)
        z_first = make_z(0)
        for t in range(PACK):
            weigh_far(t, 1)
        z_q = [quantise("z0", z_first, CHUNK)]
        z_q.append(quantise("z1", make_z(1), CHUNK))

        def project(t, chunks, dst):
            acc = bank()
            for c in chunks:
                product(acc[:, chunk(c)], w3_q, t, z_q[c])
            nc.scalar.copy(out=dst, in_=acc[:, chunks[0] * CHUNK:(chunks[-1] + 1) * CHUNK])

        def write_page(t, start, count, src):
            nc.vector.tensor_copy(page[t][:].indirect(entries(n3_list, start, count)), src)

        early = near[:, 1, 0, :]
        project(EARLY_TILE, (0,), early)
        write_page(EARLY_TILE, 0, CHUNK, early)
        for t in range(PACK):
            chunks = (1,) if t == EARLY_TILE else (0, 1)
            start = chunks[0] * CHUNK
            h = sbuf("h%d" % t, [P, S], F32)
            project(t, chunks, h[:, start:S])
            write_page(t, start, S - start, h[:, start:S])

        out_tiles = out.rearrange("(p t) w -> t p w", t=PACK)

        def fetch_on_scalar(t, start, count):
            res = sbuf("res%d_%d" % (t, start), [P, count], F32)
            nc.scalar.activation(res[:], page[t][:].indirect(entries(n4_list, start, count)), ACT.Copy, scale=-0.5)
            return res

        for t in range(PACK - 1):
            for start in range(0, U, U // 2):
                slots = slice(start, start + U // 2)
                res = fetch_on_scalar(t, start, U // 2)
                nc.gpsimd.tensor_tensor(res[:], res[:], page[t][:, slots], ALU.add)
                nc.sync.dma_start(out=out_tiles[t][:, slots], in_=res[:])
        last = PACK - 1
        for start in range(0, U, U // 4):
            slots = slice(start, start + U // 4)
            if start < U // 2:
                res = fetch_on_scalar(last, start, U // 4)
                nc.vector.tensor_tensor(res[:], res[:], page[last][:, slots], ALU.add)
            else:
                res = sbuf("res%d_%d" % (last, start), [P, U // 4], F32)
                nc.vector.tensor_copy(res[:], page[last][:].indirect(entries(n4_list, start, U // 4)))
                nc.vector.scalar_tensor_tensor(res[:], res[:], -0.5, page[last][:, slots], ALU.mult, ALU.add)
            nc.scalar.dma_start(out=out_tiles[last][:, slots], in_=res[:])
